import numpy as np
import ml_dtypes


def mxq(x, axis, fmt="e4m3"):
    dtype, down = {"e4m3": (ml_dtypes.float8_e4m3fn, 7), "e5m2": (ml_dtypes.float8_e5m2, 14)}[fmt]
    v = np.moveaxis(np.asarray(x, np.float32).astype(ml_dtypes.bfloat16).astype(np.float64), axis, -1)
    blocks = v.reshape(v.shape[:-1] + (-1, 32))
    amax = np.abs(blocks).max(-1, keepdims=True)
    byte = np.maximum(np.where(amax > 0, np.frexp(amax)[1] - 1 + 127, 0) - down, 1)
    scale = np.exp2(byte - 127.0)
    codes = (blocks / scale).astype(np.float32).astype(dtype).astype(np.float64)
    return np.moveaxis((codes * scale).reshape(v.shape), -1, axis)


WIDE = False


def mx_kscale(k):
    if not WIDE:
        return np.ones(k)
    levels = np.array([10, -10, 5, -5, 0])
    if k % 512:
        return np.exp2(np.random.permutation(np.resize(levels, k // 32))).repeat(32)
    a = np.empty((k // 512, 16))
    for p in range(k // 512):
        a[p, :8] = np.random.permutation(np.resize(levels, 8))
        for g in range(8):
            far = levels[np.abs(levels - a[p, g]) >= 10]
            a[p, g + 8] = far[np.random.randint(len(far))]
    return np.exp2(a.ravel()).repeat(32)


def f64(x):
    return np.asarray(x).astype(np.float64)


def striped(idx):
    return np.tile(idx.reshape(-1, 16).T, (8, 1)).astype(np.uint16)


def unstriped(offs):
    return offs[:16].T.reshape(-1).astype(np.int64)


def pack_weight(w):
    k, n = w.shape
    w = f64(np.asarray(w, np.float32).astype(ml_dtypes.bfloat16)).reshape(k // 32, 32, n)
    amax = np.abs(w).max(1)
    byte = np.clip(np.where(amax > 0, np.frexp(amax)[1] - 1 + 127 - 7, 1), 1, 254)
    scaled = (w * np.exp2(127.0 - byte)[:, None, :]).reshape(k, n).astype(np.float32)
    words = np.ascontiguousarray(scaled.reshape(k // 512, 128, 4, n).transpose(0, 1, 3, 2)).astype(ml_dtypes.float8_e4m3fn).view(np.uint8)
    return words, np.ascontiguousarray(byte.astype(np.uint8).reshape(k // 512, 16, n))


def unpack_weight(words, scales):
    g, p, n, _ = words.shape
    vals = np.ascontiguousarray(words).view(ml_dtypes.float8_e4m3fn).astype(np.float64) * np.repeat(np.exp2(scales.astype(np.float64) - 127.0), 8, axis=1)[..., None]
    return vals.transpose(0, 1, 3, 2).reshape(g * 512, n)


def planes(y):
    n, m = y.shape
    v = y.astype(np.float32).astype(ml_dtypes.bfloat16).astype(np.float64).reshape(n // 32, 32, m)
    top = np.abs(v).max(1)
    byte = np.clip(np.where(top > 0, np.frexp(top)[1] - 1 + 127 - 7, 1), 1, 254)
    codes = (v * np.exp2(127.0 - byte)[:, None, :]).reshape(n, m).astype(np.float32).astype(ml_dtypes.float8_e4m3fn).view(np.uint8)
    words = codes.reshape(n // 512, 128, 4, m).transpose(0, 1, 3, 2)
    return np.ascontiguousarray(words), np.ascontiguousarray(byte.astype(np.uint8).reshape(n // 512, 16, m))


def silu(v):
    return v / (1.0 + np.exp(-np.maximum(v, -700.0)))


K, T, S, W, N = 512, 2048, 512, 1024, 512


def setup_inputs():
    n = np.random.standard_normal
    s = mx_kscale(K)[:, None]
    packed_xT = pack_weight(n((K, T)) * s)
    packed_eT = pack_weight(n((K, W)) * s)
    return {
        "x_words": packed_xT[0],
        "x_scales": packed_xT[1],
        "e_words": packed_eT[0],
        "e_scales": packed_eT[1],
        "w1": (n((K, N)) / np.sqrt(2 * K) / s).astype(np.float32),
        "w2": (n((K, N)) / np.sqrt(2 * K) / s).astype(np.float32),
        "w3": (n((K, N)) / np.sqrt(2 * K) / s).astype(np.float32),
        "w4": (n((K, N)) / np.sqrt(2 * K) / s).astype(np.float32),
        "offs": striped(np.random.permutation(T)[:S]),
        "tok": striped(np.random.permutation(W)[:S]),
    }


def reference(x_words, x_scales, e_words, e_scales, w1, w2, w3, w4, offs, tok):
    xq = unpack_weight(x_words, x_scales)[:, unstriped(offs)]
    e_tok = unpack_weight(e_words, e_scales)[:, unstriped(tok)]
    g = silu(mxq(f64(w1), 0, "e4m3").T @ xq + mxq(f64(w2), 0, "e4m3").T @ e_tok)
    y = mxq(f64(w3), 0, "e4m3").T @ xq + mxq(f64(w4), 0, "e4m3").T @ e_tok
    out_0 = g * y
    return (out_0,) + planes(out_0)

@@ -1,0 +1,187 @@
+from contextlib import ExitStack
+
+import concourse.mybir as mybir
+
+K, T, S, W, N = 512, 2048, 512, 1024, 512
+FLOPS = 4 * 2 * K * N * S
+
+F32 = mybir.dt.float32
+BF16 = mybir.dt.bfloat16
+I32 = mybir.dt.int32
+U32 = mybir.dt.uint32
+U16 = mybir.dt.uint16
+U8 = mybir.dt.uint8
+FP8X4 = mybir.dt.float8_e4m3fn_x4
+SILU = mybir.ActivationFunctionType.Silu
+MULT = mybir.AluOpType.mult
+
+P = 128
+PACK = 4
+HALF = 256
+E_PLANE = 4
+
+
+def tile_picked_zmtp_silu_po_kernel(
+    tc, x_words, x_scales, e_words, e_scales, w1, w2, w3, w4, offs, tok, out_0, out_1, out_2
+):
+    nc = tc.nc
+    with ExitStack() as ctx:
+        sb = ctx.enter_context(tc.tile_pool(name="sb", bufs=1))
+        ps = ctx.enter_context(tc.psum_pool(name="ps", bufs=1))
+
+        def tile(name, shape, dtype):
+            return sb.tile(shape, dtype, name=name, align_bytes=64)
+
+        offs_sb = sb.tile([P, S // 16], U16, name="offs_sb")
+        tok_sb = sb.tile([P, S // 16], U16, name="tok_sb")
+        x_table = tile("x_table", [P, T], I32)
+        e_table = tile("e_table", [P, W], I32)
+        xs_table = tile("xs_table", [P, T], U8)
+        es_table = tile("es_table", [P, W], U8)
+        x_codes = tile("x_codes", [P, S], U32)
+        e_codes = tile("e_codes", [P, S], U32)
+        x_bytes = tile("x_bytes", [P, S], U8)
+        e_bytes = tile("e_bytes", [P, S], U8)
+
+        nc.vector.memset(es_table[:].bitcast(I32), 0)
+        nc.vector.memset(xs_table[:].bitcast(I32), 0)
+        warm_in = tile("warm_in", [P, 1], F32)
+        warm_out = tile("warm_out", [P, 1], F32)
+        nc.gpsimd.memset(warm_in[:], 0.0)
+        nc.scalar.activation(out=warm_out[:], in_=warm_in[:], func=SILU)
+
+        def load_words(table, words):
+            nc.sync.dma_start(out=table[:], in_=words[0].rearrange("p c r -> p (c r)").bitcast(I32))
+
+        def load_scale_rows(table, scales, first):
+            for r in range(4):
+                nc.sync.dma_start(
+                    out=table[first + r : P : 32, :].bitcast(I32), in_=scales[0, r:16:4, :].bitcast(I32)
+                )
+
+        def load_weight(name, w, c0, c1):
+            raw = tile(name, [P, PACK, c1 - c0], F32)
+            nc.sync.dma_start(out=raw[:], in_=w.rearrange("(p j) c -> p j c", j=PACK)[:, :, c0:c1])
+            return raw
+
+        load_words(e_table, e_words)
+        nc.sync.dma_start(tok_sb[:], tok)
+        load_scale_rows(es_table, e_scales, E_PLANE)
+        raw2 = load_weight("raw2", w2, 0, 512)
+        nc.sync.dma_start(offs_sb[:], offs)
+        load_scale_rows(xs_table, x_scales, 0)
+        raw1 = load_weight("raw1", w1, 0, 512)
+        load_words(x_table, x_words)
+        raw3a = load_weight("raw3a", w3, 0, 256)
+        raw3b = load_weight("raw3b", w3, 256, 512)
+        raw4a = load_weight("raw4a", w4, 0, 256)
+        raw4b = load_weight("raw4b", w4, 256, 384)
+        raw4c = load_weight("raw4c", w4, 384, 512)
+
+        def deal(copy, grouped, raw, m0):
+            width = raw.shape[2] // PACK
+            copy(
+                out=grouped[:, :, m0 : m0 + width, :].rearrange("p t m j -> p m j t"),
+                in_=raw.rearrange("p j (m t) -> p m j t", t=PACK),
+            )
+
+        def quantize(codes, scales, grouped):
+            nc.vector.quantize_mx(out=codes.bitcast(FP8X4), scales=scales, in_=grouped)
+
+        codes = [tile("codes%d" % i, [P, N], U32) for i in range(4)]
+        scales = [tile("scales%d" % i, [P, N], U8) for i in range(4)]
+        grouped = [tile("grouped%d" % i, [P, PACK, P, PACK], BF16) for i in range(3)]
+        grouped4 = [tile("grouped4%d" % h, [P, PACK, P // 2, PACK], BF16) for h in range(2)]
+
+        def quantize_whole(i):
+            quantize(codes[i][:], scales[i][:], grouped[i][:].rearrange("p t m j -> p (t m j)"))
+
+        def quantize_w4(h, t):
+            cols = slice(P * t + 64 * h, P * t + 64 * (h + 1))
+            quantize(codes[3][:, cols], scales[3][:, cols], grouped4[h][:, t].rearrange("p m j -> p (m j)"))
+
+        def product(acc, i, t, cols, first):
+            on_x = i % 2 == 0
+            m_cols = slice(P * t, P * (t + 1))
+            rhs = x_codes[:, cols] if on_x else e_codes[:, cols]
+            rhs_scale = x_bytes[:, cols] if on_x else e_bytes[E_PLANE:P, cols]
+            nc.tensor.matmul_mx(
+                out=acc,
+                lhsT=codes[i][:, m_cols].bitcast(FP8X4),
+                lhsT_scale=scales[i][:, m_cols],
+                rhs=rhs.bitcast(FP8X4),
+                rhs_scale=rhs_scale,
+                start=first,
+                stop=not first,
+            )
+
+        nc.vector.tensor_copy(e_codes[:], e_table[:].bitcast(U32).indirect(tok_sb[:]))
+        nc.vector.tensor_copy(e_bytes[:], es_table[:].indirect(tok_sb[:]))
+        deal(nc.scalar.copy, grouped[1], raw2[:, :, 0:256], 0)
+        deal(nc.vector.tensor_copy, grouped[1], raw2[:, :, 256:512], 64)
+        quantize_whole(1)
+        nc.vector.tensor_copy(x_bytes[:], xs_table[:].indirect(offs_sb[:]))
+        gate_acc = [ps.tile([P, S], F32, name="gate_acc%d" % t, tag="low%d" % t) for t in range(PACK)]
+        for t in range(PACK):
+            product(gate_acc[t][:], 1, t, slice(0, S), True)
+        deal(nc.scalar.copy, grouped[0], raw1[:, :, 0:256], 0)
+        deal(nc.vector.tensor_copy, grouped[0], raw1[:, :, 256:512], 64)
+        quantize_whole(0)
+        nc.vector.tensor_copy(x_codes[:], x_table[:].bitcast(U32).indirect(offs_sb[:]))
+        gate = [tile("gate%d" % t, [P, S], F32) for t in range(PACK)]
+        for t in range(PACK):
+            product(gate_acc[t][:], 0, t, slice(0, S), False)
+            nc.scalar.activation(out=gate[t][:], in_=gate_acc[t][:], func=SILU)
+
+        deal(nc.vector.tensor_copy, grouped[2], raw3a[:], 0)
+        deal(nc.vector.tensor_copy, grouped[2], raw3b[:], 64)
+        quantize_whole(2)
+        value_acc = [
+            [ps.tile([P, HALF], F32, name="value_acc%d%d" % (h, t), tag=("high%d", "low%d")[h] % t) for t in range(PACK)]
+            for h in range(2)
+        ]
+        for h in range(2):
+            for t in range(PACK):
+                product(value_acc[h][t][:], 2, t, slice(HALF * h, HALF * (h + 1)), True)
+        deal(nc.vector.tensor_copy, grouped4[0], raw4a[:], 0)
+        for t in range(PACK):
+            quantize_w4(0, t)
+        deal(nc.scalar.copy, grouped4[1], raw4b[:], 0)
+        deal(nc.vector.tensor_copy, grouped4[1], raw4c[:], 32)
+        for t in range(PACK):
+            quantize_w4(1, t)
+        for h in range(2):
+            for t in range(PACK):
+                product(value_acc[h][t][:], 3, t, slice(HALF * h, HALF * (h + 1)), False)
+
+        pieces = [(0, 256), (256, 384), (384, 512)]
+        out_codes = tile("out_codes", [P, S], U32)
+        out_scales = tile("out_scales", [P, S], U8)
+        out_rows = out_0.rearrange("(p t) j -> p t j", t=PACK)
+        out_words = out_1[0].rearrange("p c r -> p (c r)").bitcast(I32)
+        rounded = []
+        for n, (j0, j1) in enumerate(pieces):
+            h = j0 // HALF
+            result = tile("result%d" % n, [P, PACK, j1 - j0], F32)
+            for t in range(PACK):
+                nc.vector.tensor_tensor(
+                    out=result[:, t, :],
+                    in0=value_acc[h][t][:, j0 - HALF * h : j1 - HALF * h],
+                    in1=gate[t][:, j0:j1],
+                    op=MULT,
+                )
+            nc.sync.dma_start(out=out_rows[:, :, j0:j1], in_=result[:])
+            rounded.append(tile("rounded%d" % n, [P, j1 - j0, PACK], BF16))
+            copy = nc.vector.tensor_copy if n == len(pieces) - 1 else nc.scalar.copy
+            copy(
+                out=rounded[n][:].rearrange("p (c i) t -> p c t i", i=4),
+                in_=result[:].rearrange("p t (c i) -> p c t i", i=4),
+            )
+        for n, (j0, j1) in enumerate(pieces):
+            quantize(out_codes[:, j0:j1], out_scales[:, j0:j1], rounded[n][:].rearrange("p j t -> p (j t)"))
+        for h in range(2):
+            cols = slice(HALF * h, HALF * (h + 1))
+            nc.sync.dma_start(out=out_words[:, cols], in_=out_codes[:, cols].bitcast(I32))
+        for r in range(4):
+            queue = nc.scalar if r % 2 else nc.sync
+            queue.dma_start(out=out_2[0, r:16:4, :].bitcast(I32), in_=out_scales[r:P:32, :].bitcast(I32))

@@ -19,6 +19,8 @@ P = 128
 PACK = 4
 HALF = 256
 E_PLANE = 4
+EARLY = 288
+LATE = 176
 
 
 def tile_picked_zmtp_silu_po_kernel(
@@ -72,17 +74,14 @@ def tile_picked_zmtp_silu_po_kernel(
         load_scale_rows(xs_table, x_scales, 0)
         raw1 = load_weight("raw1", w1, 0, 512)
         load_words(x_table, x_words)
-        raw3a = load_weight("raw3a", w3, 0, 256)
-        raw3b = load_weight("raw3b", w3, 256, 512)
-        raw4a = load_weight("raw4a", w4, 0, 256)
-        raw4b = load_weight("raw4b", w4, 256, 384)
-        raw4c = load_weight("raw4c", w4, 384, 512)
+        raw3 = load_weight("raw3", w3, 0, 512)
+        raw4 = load_weight("raw4", w4, 0, 512)
 
-        def deal(copy, grouped, raw, m0):
-            width = raw.shape[2] // PACK
+        def deal(copy, grouped, raw, c0, c1, j0=0):
+            rows = raw.shape[1]
             copy(
-                out=grouped[:, :, m0 : m0 + width, :].rearrange("p t m j -> p m j t"),
-                in_=raw.rearrange("p j (m t) -> p m j t", t=PACK),
+                out=grouped[:, :, c0 // PACK : c1 // PACK, j0 : j0 + rows].rearrange("p t m j -> p m j t"),
+                in_=raw[:, :, c0:c1].rearrange("p j (m t) -> p m j t", t=PACK),
             )
 
         def quantize(codes, scales, grouped):
@@ -90,15 +89,14 @@ def tile_picked_zmtp_silu_po_kernel(
 
         codes = [tile("codes%d" % i, [P, N], U32) for i in range(4)]
         scales = [tile("scales%d" % i, [P, N], U8) for i in range(4)]
-        grouped = [tile("grouped%d" % i, [P, PACK, P, PACK], BF16) for i in range(3)]
-        grouped4 = [tile("grouped4%d" % h, [P, PACK, P // 2, PACK], BF16) for h in range(2)]
+        grouped = [tile("grouped%d" % i, [P, PACK, P, PACK], BF16) for i in range(4)]
 
         def quantize_whole(i):
             quantize(codes[i][:], scales[i][:], grouped[i][:].rearrange("p t m j -> p (t m j)"))
 
-        def quantize_w4(h, t):
-            cols = slice(P * t + 64 * h, P * t + 64 * (h + 1))
-            quantize(codes[3][:, cols], scales[3][:, cols], grouped4[h][:, t].rearrange("p m j -> p (m j)"))
+        def quantize_tile(i, t):
+            cols = slice(P * t, P * (t + 1))
+            quantize(codes[i][:, cols], scales[i][:, cols], grouped[i][:, t].rearrange("p m j -> p (m j)"))
 
         def product(acc, i, t, cols, first):
             on_x = i % 2 == 0
@@ -117,42 +115,46 @@ def tile_picked_zmtp_silu_po_kernel(
 
         nc.vector.tensor_copy(e_codes[:], e_table[:].bitcast(U32).indirect(tok_sb[:]))
         nc.vector.tensor_copy(e_bytes[:], es_table[:].indirect(tok_sb[:]))
-        deal(nc.scalar.copy, grouped[1], raw2[:, :, 0:256], 0)
-        deal(nc.vector.tensor_copy, grouped[1], raw2[:, :, 256:512], 64)
+        deal(nc.scalar.copy, grouped[1], raw2, 0, EARLY)
+        deal(nc.vector.tensor_copy, grouped[1], raw2, EARLY, N)
         quantize_whole(1)
         nc.vector.tensor_copy(x_bytes[:], xs_table[:].indirect(offs_sb[:]))
-        gate_acc = [ps.tile([P, S], F32, name="gate_acc%d" % t, tag="low%d" % t) for t in range(PACK)]
-        for t in range(PACK):
-            product(gate_acc[t][:], 1, t, slice(0, S), True)
-        deal(nc.scalar.copy, grouped[0], raw1[:, :, 0:256], 0)
-        deal(nc.vector.tensor_copy, grouped[0], raw1[:, :, 256:512], 64)
-        quantize_whole(0)
-        nc.vector.tensor_copy(x_codes[:], x_table[:].bitcast(U32).indirect(offs_sb[:]))
-        gate = [tile("gate%d" % t, [P, S], F32) for t in range(PACK)]
-        for t in range(PACK):
-            product(gate_acc[t][:], 0, t, slice(0, S), False)
-            nc.scalar.activation(out=gate[t][:], in_=gate_acc[t][:], func=SILU)
+        halves = [slice(0, HALF), slice(HALF, S)]
 
-        deal(nc.vector.tensor_copy, grouped[2], raw3a[:], 0)
-        deal(nc.vector.tensor_copy, grouped[2], raw3b[:], 64)
-        quantize_whole(2)
-        value_acc = [
-            [ps.tile([P, HALF], F32, name="value_acc%d%d" % (h, t), tag=("high%d", "low%d")[h] % t) for t in range(PACK)]
-            for h in range(2)
-        ]
+        def banks(name):
+            return [
+                [ps.tile([P, HALF], F32, name="%s%d%d" % (name, h, t), tag="bank%d%d" % (h, t)) for t in range(PACK)]
+                for h in range(2)
+            ]
+
+        gate_acc = banks("gate_acc")
         for h in range(2):
             for t in range(PACK):
-                product(value_acc[h][t][:], 2, t, slice(HALF * h, HALF * (h + 1)), True)
-        deal(nc.vector.tensor_copy, grouped4[0], raw4a[:], 0)
+                product(gate_acc[h][t][:], 1, t, halves[h], True)
+        deal(nc.scalar.copy, grouped[0], raw1, 0, EARLY)
+        deal(nc.vector.tensor_copy, grouped[0], raw1, EARLY, N)
+        quantize_whole(0)
+        gate = [[tile("gate%d%d" % (h, t), [P, HALF], F32) for t in range(PACK)] for h in range(2)]
+        for h in range(2):
+            nc.vector.tensor_copy(
+                x_codes[:, halves[h]], x_table[:].bitcast(U32).indirect(offs_sb[:, 16 * h : 16 * (h + 1)])
+            )
+            for t in range(PACK):
+                product(gate_acc[h][t][:], 0, t, halves[h], False)
+                nc.scalar.activation(out=gate[h][t][:], in_=gate_acc[h][t][:], func=SILU)
+        deal(nc.vector.tensor_copy, grouped[2], raw3, 0, N)
+        value_acc = banks("value_acc")
         for t in range(PACK):
-            quantize_w4(0, t)
-        deal(nc.scalar.copy, grouped4[1], raw4b[:], 0)
-        deal(nc.vector.tensor_copy, grouped4[1], raw4c[:], 32)
+            quantize_tile(2, t)
+            for h in range(2):
+                product(value_acc[h][t][:], 2, t, halves[h], True)
+        deal(nc.scalar.copy, grouped[3], raw4, 0, LATE)
+        deal(nc.vector.tensor_copy, grouped[3], raw4, LATE, N)
         for t in range(PACK):
-            quantize_w4(1, t)
+            quantize_tile(3, t)
         for h in range(2):
             for t in range(PACK):
-                product(value_acc[h][t][:], 3, t, slice(HALF * h, HALF * (h + 1)), False)
+                product(value_acc[h][t][:], 3, t, halves[h], False)
 
         pieces = [(0, 256), (256, 384), (384, 512)]
         out_codes = tile("out_codes", [P, S], U32)
@@ -167,7 +169,7 @@ def tile_picked_zmtp_silu_po_kernel(
                 nc.vector.tensor_tensor(
                     out=result[:, t, :],
                     in0=value_acc[h][t][:, j0 - HALF * h : j1 - HALF * h],
-                    in1=gate[t][:, j0:j1],
+                    in1=gate[h][t][:, j0 - HALF * h : j1 - HALF * h],
                     op=MULT,
                 )
             nc.sync.dma_start(out=out_rows[:, :, j0:j1], in_=result[:])

@@ -19,7 +19,9 @@ P = 128
 PACK = 4
 HALF = 256
 E_PLANE = 4
-EARLY = 288
+EARLY = 320
+MID = 224
+LAST = 112
 LATE = 176
 
 
@@ -70,9 +72,9 @@ def tile_picked_zmtp_silu_po_kernel(
         nc.sync.dma_start(tok_sb[:], tok)
         load_scale_rows(es_table, e_scales, E_PLANE)
         raw2 = load_weight("raw2", w2, 0, 512)
+        raw1 = load_weight("raw1", w1, 0, 512)
         nc.sync.dma_start(offs_sb[:], offs)
         load_scale_rows(xs_table, x_scales, 0)
-        raw1 = load_weight("raw1", w1, 0, 512)
         load_words(x_table, x_words)
         raw3 = load_weight("raw3", w3, 0, 512)
         raw4 = load_weight("raw4", w4, 0, 512)
@@ -118,7 +120,6 @@ def tile_picked_zmtp_silu_po_kernel(
         deal(nc.scalar.copy, grouped[1], raw2, 0, EARLY)
         deal(nc.vector.tensor_copy, grouped[1], raw2, EARLY, N)
         quantize_whole(1)
-        nc.vector.tensor_copy(x_bytes[:], xs_table[:].indirect(offs_sb[:]))
         halves = [slice(0, HALF), slice(HALF, S)]
 
         def banks(name):
@@ -131,8 +132,9 @@ def tile_picked_zmtp_silu_po_kernel(
         for h in range(2):
             for t in range(PACK):
                 product(gate_acc[h][t][:], 1, t, halves[h], True)
-        deal(nc.scalar.copy, grouped[0], raw1, 0, EARLY)
-        deal(nc.vector.tensor_copy, grouped[0], raw1, EARLY, N)
+        deal(nc.scalar.copy, grouped[0], raw1, 0, MID)
+        deal(nc.vector.tensor_copy, grouped[0], raw1, MID, N)
+        nc.vector.tensor_copy(x_bytes[:], xs_table[:].indirect(offs_sb[:]))
         quantize_whole(0)
         gate = [[tile("gate%d%d" % (h, t), [P, HALF], F32) for t in range(PACK)] for h in range(2)]
         for h in range(2):
@@ -156,34 +158,32 @@ def tile_picked_zmtp_silu_po_kernel(
             for t in range(PACK):
                 product(value_acc[h][t][:], 3, t, halves[h], False)
 
-        pieces = [(0, 256), (256, 384), (384, 512)]
         out_codes = tile("out_codes", [P, S], U32)
         out_scales = tile("out_scales", [P, S], U8)
         out_rows = out_0.rearrange("(p t) j -> p t j", t=PACK)
         out_words = out_1[0].rearrange("p c r -> p (c r)").bitcast(I32)
-        rounded = []
-        for n, (j0, j1) in enumerate(pieces):
-            h = j0 // HALF
-            result = tile("result%d" % n, [P, PACK, j1 - j0], F32)
-            for t in range(PACK):
-                nc.vector.tensor_tensor(
-                    out=result[:, t, :],
-                    in0=value_acc[h][t][:, j0 - HALF * h : j1 - HALF * h],
-                    in1=gate[h][t][:, j0 - HALF * h : j1 - HALF * h],
-                    op=MULT,
-                )
-            nc.sync.dma_start(out=out_rows[:, :, j0:j1], in_=result[:])
-            rounded.append(tile("rounded%d" % n, [P, j1 - j0, PACK], BF16))
-            copy = nc.vector.tensor_copy if n == len(pieces) - 1 else nc.scalar.copy
+
+        def weave(copy, rounded, result, j0, j1):
             copy(
-                out=rounded[n][:].rearrange("p (c i) t -> p c t i", i=4),
-                in_=result[:].rearrange("p t (c i) -> p c t i", i=4),
+                out=rounded[:, j0:j1, :].rearrange("p (c i) t -> p c t i", i=4),
+                in_=result[:, :, j0:j1].rearrange("p t (c i) -> p c t i", i=4),
             )
-        for n, (j0, j1) in enumerate(pieces):
-            quantize(out_codes[:, j0:j1], out_scales[:, j0:j1], rounded[n][:].rearrange("p j t -> p (j t)"))
+
+        rounded = [tile("rounded%d" % h, [P, HALF, PACK], BF16) for h in range(2)]
         for h in range(2):
-            cols = slice(HALF * h, HALF * (h + 1))
-            nc.sync.dma_start(out=out_words[:, cols], in_=out_codes[:, cols].bitcast(I32))
+            result = tile("result%d" % h, [P, PACK, HALF], F32)
+            for t in range(PACK):
+                nc.vector.tensor_tensor(out=result[:, t, :], in0=value_acc[h][t][:], in1=gate[h][t][:], op=MULT)
+                if t % 2:
+                    nc.sync.dma_start(out=out_rows[:, t - 1 : t + 1, halves[h]], in_=result[:, t - 1 : t + 1, :])
+            if h == 0:
+                weave(nc.scalar.copy, rounded[h], result, 0, HALF)
+            else:
+                weave(nc.scalar.copy, rounded[h], result, 0, LAST)
+                weave(nc.vector.tensor_copy, rounded[h], result, LAST, HALF)
+        for h in range(2):
+            quantize(out_codes[:, halves[h]], out_scales[:, halves[h]], rounded[h][:].rearrange("p j t -> p (j t)"))
+            nc.sync.dma_start(out=out_words[:, halves[h]], in_=out_codes[:, halves[h]].bitcast(I32))
         for r in range(4):
-            queue = nc.scalar if r % 2 else nc.sync
+            queue = nc.sync if r == 3 else nc.scalar
             queue.dma_start(out=out_2[0, r:16:4, :].bitcast(I32), in_=out_scales[r:P:32, :].bitcast(I32))

from contextlib import ExitStack

import concourse.mybir as mybir

K, T, S, W, N = 512, 2048, 512, 1024, 512
FLOPS = 4 * 2 * K * N * S

F32 = mybir.dt.float32
BF16 = mybir.dt.bfloat16
I32 = mybir.dt.int32
U32 = mybir.dt.uint32
U16 = mybir.dt.uint16
U8 = mybir.dt.uint8
FP8X4 = mybir.dt.float8_e4m3fn_x4
SILU = mybir.ActivationFunctionType.Silu
MULT = mybir.AluOpType.mult

P = 128
PACK = 4
HALF = 256
E_PLANE = 4
EARLY = 320
MID = 224
LAST = 112
LATE = 176


def tile_picked_zmtp_silu_po_kernel(
    tc, x_words, x_scales, e_words, e_scales, w1, w2, w3, w4, offs, tok, out_0, out_1, out_2
):
    nc = tc.nc
    with ExitStack() as ctx:
        sb = ctx.enter_context(tc.tile_pool(name="sb", bufs=1))
        ps = ctx.enter_context(tc.psum_pool(name="ps", bufs=1))

        def tile(name, shape, dtype):
            return sb.tile(shape, dtype, name=name, align_bytes=64)

        offs_sb = sb.tile([P, S // 16], U16, name="offs_sb")
        tok_sb = sb.tile([P, S // 16], U16, name="tok_sb")
        x_table = tile("x_table", [P, T], I32)
        e_table = tile("e_table", [P, W], I32)
        xs_table = tile("xs_table", [P, T], U8)
        es_table = tile("es_table", [P, W], U8)
        x_codes = tile("x_codes", [P, S], U32)
        e_codes = tile("e_codes", [P, S], U32)
        x_bytes = tile("x_bytes", [P, S], U8)
        e_bytes = tile("e_bytes", [P, S], U8)

        nc.vector.memset(es_table[:].bitcast(I32), 0)
        nc.vector.memset(xs_table[:].bitcast(I32), 0)
        warm_in = tile("warm_in", [P, 1], F32)
        warm_out = tile("warm_out", [P, 1], F32)
        nc.gpsimd.memset(warm_in[:], 0.0)
        nc.scalar.activation(out=warm_out[:], in_=warm_in[:], func=SILU)

        def load_words(table, words):
            nc.sync.dma_start(out=table[:], in_=words[0].rearrange("p c r -> p (c r)").bitcast(I32))

        def load_scale_rows(table, scales, first):
            for r in range(4):
                nc.sync.dma_start(
                    out=table[first + r : P : 32, :].bitcast(I32), in_=scales[0, r:16:4, :].bitcast(I32)
                )

        def load_weight(name, w, c0, c1):
            raw = tile(name, [P, PACK, c1 - c0], F32)
            nc.sync.dma_start(out=raw[:], in_=w.rearrange("(p j) c -> p j c", j=PACK)[:, :, c0:c1])
            return raw

        load_words(e_table, e_words)
        nc.sync.dma_start(tok_sb[:], tok)
        load_scale_rows(es_table, e_scales, E_PLANE)
        raw2 = load_weight("raw2", w2, 0, 512)
        raw1 = load_weight("raw1", w1, 0, 512)
        nc.sync.dma_start(offs_sb[:], offs)
        load_scale_rows(xs_table, x_scales, 0)
        load_words(x_table, x_words)
        raw3 = load_weight("raw3", w3, 0, 512)
        raw4 = load_weight("raw4", w4, 0, 512)

        def deal(copy, grouped, raw, c0, c1, j0=0):
            rows = raw.shape[1]
            copy(
                out=grouped[:, :, c0 // PACK : c1 // PACK, j0 : j0 + rows].rearrange("p t m j -> p m j t"),
                in_=raw[:, :, c0:c1].rearrange("p j (m t) -> p m j t", t=PACK),
            )

        def quantize(codes, scales, grouped):
            nc.vector.quantize_mx(out=codes.bitcast(FP8X4), scales=scales, in_=grouped)

        codes = [tile("codes%d" % i, [P, N], U32) for i in range(4)]
        scales = [tile("scales%d" % i, [P, N], U8) for i in range(4)]
        grouped = [tile("grouped%d" % i, [P, PACK, P, PACK], BF16) for i in range(4)]

        def quantize_whole(i):
            quantize(codes[i][:], scales[i][:], grouped[i][:].rearrange("p t m j -> p (t m j)"))

        def quantize_tile(i, t):
            cols = slice(P * t, P * (t + 1))
            quantize(codes[i][:, cols], scales[i][:, cols], grouped[i][:, t].rearrange("p m j -> p (m j)"))

        def product(acc, i, t, cols, first):
            on_x = i % 2 == 0
            m_cols = slice(P * t, P * (t + 1))
            rhs = x_codes[:, cols] if on_x else e_codes[:, cols]
            rhs_scale = x_bytes[:, cols] if on_x else e_bytes[E_PLANE:P, cols]
            nc.tensor.matmul_mx(
                out=acc,
                lhsT=codes[i][:, m_cols].bitcast(FP8X4),
                lhsT_scale=scales[i][:, m_cols],
                rhs=rhs.bitcast(FP8X4),
                rhs_scale=rhs_scale,
                start=first,
                stop=not first,
            )

        nc.vector.tensor_copy(e_codes[:], e_table[:].bitcast(U32).indirect(tok_sb[:]))
        nc.vector.tensor_copy(e_bytes[:], es_table[:].indirect(tok_sb[:]))
        deal(nc.scalar.copy, grouped[1], raw2, 0, EARLY)
        deal(nc.vector.tensor_copy, grouped[1], raw2, EARLY, N)
        quantize_whole(1)
        halves = [slice(0, HALF), slice(HALF, S)]

        def banks(name):
            return [
                [ps.tile([P, HALF], F32, name="%s%d%d" % (name, h, t), tag="bank%d%d" % (h, t)) for t in range(PACK)]
                for h in range(2)
            ]

        gate_acc = banks("gate_acc")
        for h in range(2):
            for t in range(PACK):
                product(gate_acc[h][t][:], 1, t, halves[h], True)
        deal(nc.scalar.copy, grouped[0], raw1, 0, MID)
        deal(nc.vector.tensor_copy, grouped[0], raw1, MID, N)
        nc.vector.tensor_copy(x_bytes[:], xs_table[:].indirect(offs_sb[:]))
        quantize_whole(0)
        gate = [[tile("gate%d%d" % (h, t), [P, HALF], F32) for t in range(PACK)] for h in range(2)]
        for h in range(2):
            nc.vector.tensor_copy(
                x_codes[:, halves[h]], x_table[:].bitcast(U32).indirect(offs_sb[:, 16 * h : 16 * (h + 1)])
            )
            for t in range(PACK):
                product(gate_acc[h][t][:], 0, t, halves[h], False)
                nc.scalar.activation(out=gate[h][t][:], in_=gate_acc[h][t][:], func=SILU)
        deal(nc.vector.tensor_copy, grouped[2], raw3, 0, N)
        value_acc = banks("value_acc")
        for t in range(PACK):
            quantize_tile(2, t)
            for h in range(2):
                product(value_acc[h][t][:], 2, t, halves[h], True)
        deal(nc.scalar.copy, grouped[3], raw4, 0, LATE)
        deal(nc.vector.tensor_copy, grouped[3], raw4, LATE, N)
        for t in range(PACK):
            quantize_tile(3, t)
        for h in range(2):
            for t in range(PACK):
                product(value_acc[h][t][:], 3, t, halves[h], False)

        out_codes = tile("out_codes", [P, S], U32)
        out_scales = tile("out_scales", [P, S], U8)
        out_rows = out_0.rearrange("(p t) j -> p t j", t=PACK)
        out_words = out_1[0].rearrange("p c r -> p (c r)").bitcast(I32)

        def weave(copy, rounded, result, j0, j1):
            copy(
                out=rounded[:, j0:j1, :].rearrange("p (c i) t -> p c t i", i=4),
                in_=result[:, :, j0:j1].rearrange("p t (c i) -> p c t i", i=4),
            )

        rounded = [tile("rounded%d" % h, [P, HALF, PACK], BF16) for h in range(2)]
        for h in range(2):
            result = tile("result%d" % h, [P, PACK, HALF], F32)
            for t in range(PACK):
                nc.vector.tensor_tensor(out=result[:, t, :], in0=value_acc[h][t][:], in1=gate[h][t][:], op=MULT)
                if t % 2:
                    nc.sync.dma_start(out=out_rows[:, t - 1 : t + 1, halves[h]], in_=result[:, t - 1 : t + 1, :])
            if h == 0:
                weave(nc.scalar.copy, rounded[h], result, 0, HALF)
            else:
                weave(nc.scalar.copy, rounded[h], result, 0, LAST)
                weave(nc.vector.tensor_copy, rounded[h], result, LAST, HALF)
        for h in range(2):
            quantize(out_codes[:, halves[h]], out_scales[:, halves[h]], rounded[h][:].rearrange("p j t -> p (j t)"))
            nc.sync.dma_start(out=out_words[:, halves[h]], in_=out_codes[:, halves[h]].bitcast(I32))
        for r in range(4):
            queue = nc.sync if r == 3 else nc.scalar
            queue.dma_start(out=out_2[0, r:16:4, :].bitcast(I32), in_=out_scales[r:P:32, :].bitcast(I32))
